import numpy as np
import ml_dtypes


def mxq(x, axis, fmt="e4m3"):
    dtype, down = {"e4m3": (ml_dtypes.float8_e4m3fn, 7), "e5m2": (ml_dtypes.float8_e5m2, 14)}[fmt]
    v = np.moveaxis(np.asarray(x, np.float32).astype(ml_dtypes.bfloat16).astype(np.float64), axis, -1)
    blocks = v.reshape(v.shape[:-1] + (-1, 32))
    amax = np.abs(blocks).max(-1, keepdims=True)
    byte = np.maximum(np.where(amax > 0, np.frexp(amax)[1] - 1 + 127, 0) - down, 1)
    scale = np.exp2(byte - 127.0)
    codes = (blocks / scale).astype(np.float32).astype(dtype).astype(np.float64)
    return np.moveaxis((codes * scale).reshape(v.shape), -1, axis)


WIDE = False


def mx_kscale(k):
    if not WIDE:
        return np.ones(k)
    levels = np.array([30, -30])
    if k % 512:
        return np.exp2(np.random.permutation(np.resize(levels, k // 32))).repeat(32)
    a = np.empty((k // 512, 16))
    for p in range(k // 512):
        a[p, :8] = np.random.permutation(np.resize(levels, 8))
        for g in range(8):
            far = levels[np.abs(levels - a[p, g]) >= 10]
            a[p, g + 8] = far[np.random.randint(len(far))]
    return np.exp2(a.ravel()).repeat(32)


def f64(x):
    return np.asarray(x).astype(np.float64)


def striped(idx):
    return np.tile(np.asarray(idx).reshape(-1, 16).T, (8, 1)).astype(np.uint16)


def unstriped(offs):
    return offs[:16].T.reshape(-1).astype(np.int64)


E2M1 = np.array([0.0, 0.5, 1.0, 1.5, 2.0, 3.0, 4.0, 6.0, -0.0, -0.5, -1.0, -1.5, -2.0, -3.0, -4.0, -6.0])


def pack_weight(w, fmt):
    k, n = w.shape
    w = f64(np.asarray(w, np.float32).astype(ml_dtypes.bfloat16)).reshape(k // 32, 32, n)
    amax = np.abs(w).max(1)
    if fmt in ("e4m3", "e5m2"):
        byte = np.frexp(amax)[1] - 1 + 127 - (7 if fmt == "e4m3" else 14)
    else:
        mant, ex = np.frexp(amax / 6.0)
        byte = np.where(mant > 0.5, ex, ex - 1) + 127
    byte = np.clip(np.where(amax > 0, byte, 1), 1, 254)
    scaled = (w * np.exp2(127.0 - byte)[:, None, :]).reshape(k, n).astype(np.float32)
    by_word = np.ascontiguousarray(scaled.reshape(k // 512, 128, 4, n).transpose(0, 1, 3, 2))
    if fmt in ("e4m3", "e5m2"):
        words = by_word.astype(ml_dtypes.float8_e4m3fn if fmt == "e4m3" else ml_dtypes.float8_e5m2).view(np.uint8)
    else:
        c = by_word.astype(ml_dtypes.float4_e2m1fn).view(np.uint8) & 0xF
        words = (c[..., 0::2] | (c[..., 1::2] << 4)).reshape(k // 512, 128, 2 * n)
    return np.ascontiguousarray(words), np.ascontiguousarray(byte.astype(np.uint8).reshape(k // 512, 16, n))


def unpack_weight(words, scales, fmt):
    g, _, n = scales.shape
    words = np.ascontiguousarray(words).reshape(g, 128, n, -1)
    if fmt in ("e4m3", "e5m2"):
        vals = words.view(ml_dtypes.float8_e4m3fn if fmt == "e4m3" else ml_dtypes.float8_e5m2).astype(np.float64)
    else:
        nib = np.empty((g, 128, n, 4), np.uint8)
        nib[..., 0::2] = words & 0xF
        nib[..., 1::2] = words >> 4
        vals = E2M1[nib]
    vals = vals * np.repeat(np.exp2(scales.astype(np.float64) - 127.0), 8, axis=1)[..., None]
    return vals.transpose(0, 1, 3, 2).reshape(g * 512, n)


K, T, J, I, V = 1024, 1024, 256, 256, 1024


def setup_inputs():
    n = np.random.standard_normal
    idx = np.random.permutation(T)[:J]
    idx2 = np.random.permutation(V)[:I]
    fk = mx_kscale(K)
    xtp = pack_weight(n((K, T)) * 0.04 * fk[:, None], "e5m2")
    return {
        "xt_words": xtp[0],
        "xt_scales": xtp[1],
        "ky": (n((K, V)) / fk[:, None]).astype(np.float32),
        "bi": (np.random.uniform(-0.7, 0.7, (1, I))).astype(np.float32),
        "pr": (np.random.uniform(0.5, 1.5, (1, I))).astype(np.float32),
        "offs": striped(idx),
        "offs2": striped(idx2),
    }


def reference(xt_words, xt_scales, ky, bi, pr, offs, offs2):
    idx = unstriped(offs)
    idx2 = unstriped(offs2)
    xtu = unpack_weight(xt_words, xt_scales, "e5m2")
    xtidxg = xtu[:, idx]
    kyidx2q = mxq(f64(ky)[:, idx2], 0, "e4m3")
    a0 = xtidxg.T @ kyidx2q
    a = a0 + f64(bi)
    e = np.exp(0.7 * a) * f64(pr)
    y = 256.0 * e / np.sum(e, axis=1, keepdims=True) - f64(pr)
    return y

@@ -1,0 +1,158 @@
+from contextlib import ExitStack
+
+import concourse.mybir as mybir
+from concourse.masks import make_identity
+
+K, T, J, I, V = 1024, 1024, 256, 256, 1024
+FLOPS = 2 * K * J * I
+
+F32 = mybir.dt.float32
+BF16 = mybir.dt.bfloat16
+I32 = mybir.dt.int32
+U32 = mybir.dt.uint32
+U16 = mybir.dt.uint16
+U8 = mybir.dt.uint8
+E4M3 = mybir.dt.float8_e4m3fn_x4
+E5M2 = mybir.dt.float8_e5m2_x4
+ALU = mybir.AluOpType
+ACT = mybir.ActivationFunctionType
+
+P = 128
+PACK = 4
+K_PASS = P * PACK
+PASSES = K // K_PASS
+BLOCKS = J // P
+GAIN = 0.7
+SHARE = 256.0
+
+
+def tile_list_scores_picked_listed_shares_kernel(tc, xt_words, xt_scales, ky, bi, pr, offs, offs2, out):
+    nc = tc.nc
+    with ExitStack() as ctx:
+        lists = ctx.enter_context(tc.tile_pool(name="lists", bufs=1))
+        keep = ctx.enter_context(tc.tile_pool(name="keep", bufs=1))
+        psum = ctx.enter_context(tc.psum_pool(name="psum", bufs=1))
+
+        token_list = lists.tile([P, J // 16], U16, name="token_list")
+        key_list = lists.tile([P, I // 16], U16, name="key_list")
+
+        token_scales = keep.tile([P, PASSES, T], U8, name="token_scales")
+        nc.vector.memset(token_scales[:].bitcast(I32), 0)
+
+        key_planes = {}
+        for z in range(PASSES):
+            rows = ky[z * K_PASS : (z + 1) * K_PASS, :].rearrange("(p t) v -> p t v", t=PACK)
+            for t in range(PACK):
+                plane = keep.tile([P, V], F32, name=f"key_plane_{z}_{t}")
+                nc.sync.dma_start(plane[:], rows[:, t, :])
+                key_planes[z, t] = plane
+                if (z, t) == (0, 0):
+                    nc.sync.dma_start(key_list[:], offs2)
+                    nc.sync.dma_start(
+                        token_scales[0:P:8, :, :].bitcast(I32),
+                        xt_scales.rearrange("z q c -> q z c").bitcast(I32),
+                    )
+                if (z, t) == (0, 1):
+                    nc.sync.dma_start(token_list[:], offs)
+        token_words = []
+        for z in range(PASSES):
+            words = keep.tile([P, T], I32, name=f"token_words_{z}")
+            nc.sync.dma_start(words[:], xt_words[z].rearrange("p c r -> p (c r)").bitcast(I32))
+            token_words.append(words)
+
+        bias_cols = keep.tile([P, 2], F32, name="bias_cols")
+        prior_cols = keep.tile([P, 2], F32, name="prior_cols")
+        nc.gpsimd.dma_start(bias_cols[:], bi.rearrange("o (p c) -> p (o c)", c=2))
+        nc.gpsimd.dma_start(prior_cols[:], pr.rearrange("o (p c) -> p (o c)", c=2))
+        identity = keep.tile([P, P], F32, name="identity")
+        make_identity(nc, identity[:])
+
+        spread = psum.tile([P, 4, P], F32, name="spread")
+        for c in range(2):
+            nc.tensor.transpose(spread[:, c, :], bias_cols[:, c : c + 1].to_broadcast([P, P]), identity[:])
+            nc.tensor.transpose(spread[:, 2 + c, :], prior_cols[:, c : c + 1].to_broadcast([P, P]), identity[:])
+        neg_bias = keep.tile([P, I], F32, name="neg_bias")
+        prior = keep.tile([P, I], F32, name="prior")
+        nc.scalar.activation(
+            neg_bias[:].rearrange("p (n c) -> p n c", c=2),
+            spread[:, 0:2, :].rearrange("p c n -> p n c"),
+            ACT.Copy,
+            scale=-GAIN,
+        )
+        nc.scalar.copy(
+            prior[:].rearrange("p (n c) -> p n c", c=2), spread[:, 2:4, :].rearrange("p c n -> p n c")
+        )
+
+        picked_scales = keep.tile([P, PASSES, J], U8, name="picked_scales")
+        scale_planes = keep.tile([P, PASSES, J], U8, name="scale_planes", align_bytes=64)
+
+        key_codes, key_scales = [], []
+        for z in range(PASSES):
+            woven = keep.tile([P, I, PACK], BF16, name=f"woven_{z}", align_bytes=64)
+            for t in range(PACK):
+                nc.vector.tensor_copy(woven[:, :, t], key_planes[z, t][:].indirect(key_list[:]))
+                if z == 0 and t in (1, 2):
+                    nc.vector.tensor_copy(
+                        picked_scales[:, t - 1, :], token_scales[:, t - 1, :].indirect(token_list[:])
+                    )
+                if (z, t) == (0, 3):
+                    nc.vector.tensor_copy(scale_planes[:].bitcast(I32), picked_scales[:].bitcast(I32))
+                    for r in range(1, 4):
+                        nc.scalar.dma_start(
+                            scale_planes[r:P:32, :, :].bitcast(I32),
+                            picked_scales[8 * r : P : 32, :, :].bitcast(I32),
+                        )
+            codes = keep.tile([P, I], U32, name=f"key_codes_{z}", align_bytes=64)
+            scales = keep.tile([P, I], U8, name=f"key_scales_{z}", align_bytes=64)
+            nc.vector.quantize_mx(
+                out=codes[:].bitcast(E4M3), scales=scales[:], in_=woven[:].rearrange("p i t -> p (i t)")
+            )
+            key_codes.append(codes)
+            key_scales.append(scales)
+
+        scores = [psum.tile([P, I], F32, name=f"scores_{b}") for b in range(BLOCKS)]
+        for z in range(PASSES):
+            for b in range(BLOCKS):
+                picked = keep.tile([P, P], U32, name=f"picked_words_{z}_{b}", align_bytes=64)
+                nc.vector.tensor_copy(
+                    picked[:], token_words[z][:].bitcast(U32).indirect(token_list[:, 8 * b : 8 * (b + 1)])
+                )
+                nc.tensor.matmul_mx(
+                    out=scores[b][:],
+                    lhsT=picked[:].bitcast(E5M2),
+                    lhsT_scale=scale_planes[:, z, b * P : (b + 1) * P],
+                    rhs=key_codes[z][:].bitcast(E4M3),
+                    rhs_scale=key_scales[z][:],
+                    start=(z == 0),
+                    stop=(z == PASSES - 1),
+                )
+
+        def per_block(name, cols):
+            return [keep.tile([P, cols], F32, name=f"{name}_{b}") for b in range(BLOCKS)]
+
+        neg_logit, least, expo, weighted, result = (
+            per_block("neg_logit", I), per_block("least", 1), per_block("expo", I),
+            per_block("weighted", I), per_block("result", I),
+        )
+        total, part, inverse = per_block("total", 1), per_block("part", 1), per_block("inverse", 1)
+        for b in range(BLOCKS):
+            nc.vector.scalar_tensor_tensor(
+                neg_logit[b][:], scores[b][:], -GAIN, neg_bias[:], ALU.mult, ALU.add
+            )
+        for b in range(BLOCKS):
+            nc.vector.tensor_reduce(least[b][:], neg_logit[b][:], mybir.AxisListType.X, ALU.min)
+        for b in range(BLOCKS):
+            nc.scalar.activation(expo[b][:], neg_logit[b][:], ACT.Exp, bias=least[b][:], scale=-1.0)
+        for b in range(BLOCKS):
+            nc.vector.scalar_tensor_tensor(
+                weighted[b][:], expo[b][:], 1.0, prior[:], ALU.mult, ALU.mult, accum_out=total[b][:]
+            )
+        for b in range(BLOCKS):
+            nc.vector.tensor_scalar(part[b][:], total[b][:], 1.0 / SHARE, None, ALU.mult)
+        for b in range(BLOCKS):
+            nc.vector.reciprocal(inverse[b][:], part[b][:])
+        for b in range(BLOCKS):
+            nc.vector.scalar_tensor_tensor(
+                result[b][:], weighted[b][:], inverse[b][:], prior[:], ALU.mult, ALU.subtract
+            )
+            nc.sync.dma_start(out[b * P : (b + 1) * P, :], result[b][:])

@@ -39,74 +39,94 @@ def tile_list_scores_picked_listed_shares_kernel(tc, xt_words, xt_scales, ky, bi
         token_scales = keep.tile([P, PASSES, T], U8, name="token_scales")
         nc.vector.memset(token_scales[:].bitcast(I32), 0)
 
+        rows_in = keep.tile([P, I], F32, name="rows_in")
+        nc.gpsimd.memset(rows_in[:], 0.0)
+
         key_planes = {}
-        for z in range(PASSES):
+        for z, t0, count in ((0, 0, 2), (0, 2, 2), (1, 0, 2), (1, 2, 1), (1, 3, 1)):
             rows = ky[z * K_PASS : (z + 1) * K_PASS, :].rearrange("(p t) v -> p t v", t=PACK)
-            for t in range(PACK):
-                plane = keep.tile([P, V], F32, name=f"key_plane_{z}_{t}")
-                nc.sync.dma_start(plane[:], rows[:, t, :])
-                key_planes[z, t] = plane
-                if (z, t) == (0, 0):
-                    nc.sync.dma_start(key_list[:], offs2)
-                    nc.sync.dma_start(
-                        token_scales[0:P:8, :, :].bitcast(I32),
-                        xt_scales.rearrange("z q c -> q z c").bitcast(I32),
-                    )
-                if (z, t) == (0, 1):
-                    nc.sync.dma_start(token_list[:], offs)
+            planes = keep.tile([P, count, V], F32, name=f"key_planes_{z}_{t0}")
+            nc.sync.dma_start(planes[:], rows[:, t0 : t0 + count, :])
+            for t in range(count):
+                key_planes[z, t0 + t] = planes[:, t, :]
+            if (z, t0) == (0, 0):
+                nc.sync.dma_start(key_list[:], offs2)
+                nc.sync.dma_start(token_list[:], offs)
+                nc.sync.dma_start(rows_in[0:1, :], bi)
+                nc.sync.dma_start(rows_in[1:2, :], pr)
+                nc.sync.dma_start(
+                    token_scales[0:P:8, :, :].bitcast(I32),
+                    xt_scales.rearrange("z q c -> q z c").bitcast(I32),
+                )
         token_words = []
         for z in range(PASSES):
             words = keep.tile([P, T], I32, name=f"token_words_{z}")
             nc.sync.dma_start(words[:], xt_words[z].rearrange("p c r -> p (c r)").bitcast(I32))
             token_words.append(words)
 
-        bias_cols = keep.tile([P, 2], F32, name="bias_cols")
-        prior_cols = keep.tile([P, 2], F32, name="prior_cols")
-        nc.gpsimd.dma_start(bias_cols[:], bi.rearrange("o (p c) -> p (o c)", c=2))
-        nc.gpsimd.dma_start(prior_cols[:], pr.rearrange("o (p c) -> p (o c)", c=2))
         identity = keep.tile([P, P], F32, name="identity")
         make_identity(nc, identity[:])
 
-        spread = psum.tile([P, 4, P], F32, name="spread")
-        for c in range(2):
-            nc.tensor.transpose(spread[:, c, :], bias_cols[:, c : c + 1].to_broadcast([P, P]), identity[:])
-            nc.tensor.transpose(spread[:, 2 + c, :], prior_cols[:, c : c + 1].to_broadcast([P, P]), identity[:])
+        turned = psum.tile([P, 2, P], F32, name="turned")
+        for h in range(2):
+            nc.tensor.transpose(turned[:, h, :], rows_in[:, h * P : (h + 1) * P], identity[:])
+        cols = keep.tile([P, 2, 2], F32, name="cols")
+        nc.scalar.activation(cols[:], turned[:, :, 0:2], ACT.Copy)
+        bias_rows = psum.tile([P, I], F32, name="bias_rows")
+        prior = psum.tile([P, I], F32, name="prior")
+        for which, spread in enumerate((bias_rows, prior)):
+            for h in range(2):
+                nc.tensor.transpose(
+                    spread[:, h * P : (h + 1) * P],
+                    cols[:, h, which : which + 1].to_broadcast([P, P]),
+                    identity[:],
+                )
         neg_bias = keep.tile([P, I], F32, name="neg_bias")
-        prior = keep.tile([P, I], F32, name="prior")
-        nc.scalar.activation(
-            neg_bias[:].rearrange("p (n c) -> p n c", c=2),
-            spread[:, 0:2, :].rearrange("p c n -> p n c"),
-            ACT.Copy,
-            scale=-GAIN,
-        )
-        nc.scalar.copy(
-            prior[:].rearrange("p (n c) -> p n c", c=2), spread[:, 2:4, :].rearrange("p c n -> p n c")
-        )
+        nc.scalar.activation(neg_bias[:], bias_rows[:], ACT.Copy, scale=-GAIN)
 
         picked_scales = keep.tile([P, PASSES, J], U8, name="picked_scales")
         scale_planes = keep.tile([P, PASSES, J], U8, name="scale_planes", align_bytes=64)
 
+        nc.gpsimd.memset(scale_planes[:].bitcast(I32), 0)
+        for z in range(PASSES):
+            nc.vector.tensor_copy(picked_scales[:, z, :], token_scales[:, z, :].indirect(token_list[:]))
+        for q in range(0, P, 32):
+            nc.vector.tensor_copy(
+                scale_planes[q : q + 1, :, :].bitcast(I32), picked_scales[q : q + 1, :, :].bitcast(I32)
+            )
+        for r in range(1, 4):
+            nc.scalar.dma_start(
+                scale_planes[r:P:32, :, :].bitcast(I32), picked_scales[8 * r : P : 32, :, :].bitcast(I32)
+            )
+
         key_codes, key_scales = [], []
         for z in range(PASSES):
             woven = keep.tile([P, I, PACK], BF16, name=f"woven_{z}", align_bytes=64)
-            for t in range(PACK):
-                nc.vector.tensor_copy(woven[:, :, t], key_planes[z, t][:].indirect(key_list[:]))
-                if z == 0 and t in (1, 2):
-                    nc.vector.tensor_copy(
-                        picked_scales[:, t - 1, :], token_scales[:, t - 1, :].indirect(token_list[:])
-                    )
-                if (z, t) == (0, 3):
-                    nc.vector.tensor_copy(scale_planes[:].bitcast(I32), picked_scales[:].bitcast(I32))
-                    for r in range(1, 4):
-                        nc.scalar.dma_start(
-                            scale_planes[r:P:32, :, :].bitcast(I32),
-                            picked_scales[8 * r : P : 32, :, :].bitcast(I32),
-                        )
+            picked_keys = keep.tile([P, PACK, I], F32, name=f"picked_keys_{z}")
             codes = keep.tile([P, I], U32, name=f"key_codes_{z}", align_bytes=64)
             scales = keep.tile([P, I], U8, name=f"key_scales_{z}", align_bytes=64)
-            nc.vector.quantize_mx(
-                out=codes[:].bitcast(E4M3), scales=scales[:], in_=woven[:].rearrange("p i t -> p (i t)")
-            )
+            last = z == PASSES - 1
+            for t in range(PACK):
+                window = key_planes[z, t]
+                if last and t == PACK - 1:
+                    nc.vector.tensor_copy(picked_keys[:, t, 0:P], window.indirect(key_list[:, 0:8]))
+                    nc.scalar.activation(picked_keys[:, t, P:I], window.indirect(key_list[:, 8:16]), ACT.Copy)
+                elif t % 2 == 0:
+                    nc.scalar.activation(picked_keys[:, t, :], window.indirect(key_list[:]), ACT.Copy)
+                else:
+                    nc.vector.tensor_copy(picked_keys[:, t, :], window.indirect(key_list[:]))
+            parts = [slice(0, P), slice(P, I)] if last else [slice(0, I)]
+            for cols_i in parts:
+                nc.vector.tensor_copy(
+                    woven[:, cols_i, :].rearrange("p (c i) t -> p c t i", i=4),
+                    picked_keys[:, :, cols_i].rearrange("p t (c i) -> p c t i", i=4),
+                )
+            for cols_i in parts:
+                nc.vector.quantize_mx(
+                    out=codes[:, cols_i].bitcast(E4M3),
+                    scales=scales[:, cols_i],
+                    in_=woven[:, cols_i, :].rearrange("p i t -> p (i t)"),
+                )
             key_codes.append(codes)
             key_scales.append(scales)
 

@@ -116,8 +116,8 @@ def tile_list_scores_picked_listed_shares_kernel(tc, xt_words, xt_scales, ky, bi
                 else:
                     nc.vector.tensor_copy(picked_keys[:, t, :], window.indirect(key_list[:]))
             parts = [slice(0, P), slice(P, I)] if last else [slice(0, I)]
-            for cols_i in parts:
-                nc.vector.tensor_copy(
+            for cols_i, weave in zip(parts, (nc.vector.tensor_copy, nc.scalar.copy)):
+                weave(
                     woven[:, cols_i, :].rearrange("p (c i) t -> p c t i", i=4),
                     picked_keys[:, :, cols_i].rearrange("p t (c i) -> p c t i", i=4),
                 )
@@ -150,11 +150,9 @@ def tile_list_scores_picked_listed_shares_kernel(tc, xt_words, xt_scales, ky, bi
         def per_block(name, cols):
             return [keep.tile([P, cols], F32, name=f"{name}_{b}") for b in range(BLOCKS)]
 
-        neg_logit, least, expo, weighted, result = (
-            per_block("neg_logit", I), per_block("least", 1), per_block("expo", I),
-            per_block("weighted", I), per_block("result", I),
-        )
-        total, part, inverse = per_block("total", 1), per_block("part", 1), per_block("inverse", 1)
+        neg_logit, least, expo = per_block("neg_logit", I), per_block("least", 1), per_block("expo", I)
+        terms, mean, inverse = per_block("terms", I), per_block("mean", 1), per_block("inverse", 1)
+        centred, result = per_block("centred", I), per_block("result", I)
         for b in range(BLOCKS):
             nc.vector.scalar_tensor_tensor(
                 neg_logit[b][:], scores[b][:], -GAIN, neg_bias[:], ALU.mult, ALU.add
@@ -165,14 +163,14 @@ def tile_list_scores_picked_listed_shares_kernel(tc, xt_words, xt_scales, ky, bi
             nc.scalar.activation(expo[b][:], neg_logit[b][:], ACT.Exp, bias=least[b][:], scale=-1.0)
         for b in range(BLOCKS):
             nc.vector.scalar_tensor_tensor(
-                weighted[b][:], expo[b][:], 1.0, prior[:], ALU.mult, ALU.mult, accum_out=total[b][:]
+                terms[b][:], expo[b][:], 1.0 / SHARE, prior[:], ALU.mult, ALU.mult, accum_out=mean[b][:]
             )
         for b in range(BLOCKS):
-            nc.vector.tensor_scalar(part[b][:], total[b][:], 1.0 / SHARE, None, ALU.mult)
-        for b in range(BLOCKS):
-            nc.vector.reciprocal(inverse[b][:], part[b][:])
-        for b in range(BLOCKS):
+            nc.vector.reciprocal(inverse[b][:], mean[b][:])
             nc.vector.scalar_tensor_tensor(
-                result[b][:], weighted[b][:], inverse[b][:], prior[:], ALU.mult, ALU.subtract
+                centred[b][:], expo[b][:], mean[b][:], prior[:], ALU.subtract, ALU.mult
             )
+        nc.scalar.activation(result[0][:], centred[0][:], ACT.Copy, scale=inverse[0][:])
+        nc.vector.tensor_scalar(result[1][:], centred[1][:], inverse[1][:], None, ALU.mult)
+        for b in range(BLOCKS):
             nc.sync.dma_start(out[b * P : (b + 1) * P, :], result[b][:])

from contextlib import ExitStack

import concourse.mybir as mybir
from concourse.masks import make_identity

K, T, J, I, V = 1024, 1024, 256, 256, 1024
FLOPS = 2 * K * J * I

F32 = mybir.dt.float32
BF16 = mybir.dt.bfloat16
I32 = mybir.dt.int32
U32 = mybir.dt.uint32
U16 = mybir.dt.uint16
U8 = mybir.dt.uint8
E4M3 = mybir.dt.float8_e4m3fn_x4
E5M2 = mybir.dt.float8_e5m2_x4
ALU = mybir.AluOpType
ACT = mybir.ActivationFunctionType

P = 128
PACK = 4
K_PASS = P * PACK
PASSES = K // K_PASS
BLOCKS = J // P
GAIN = 0.7
SHARE = 256.0


def tile_list_scores_picked_listed_shares_kernel(tc, xt_words, xt_scales, ky, bi, pr, offs, offs2, out):
    nc = tc.nc
    with ExitStack() as ctx:
        lists = ctx.enter_context(tc.tile_pool(name="lists", bufs=1))
        keep = ctx.enter_context(tc.tile_pool(name="keep", bufs=1))
        psum = ctx.enter_context(tc.psum_pool(name="psum", bufs=1))

        token_list = lists.tile([P, J // 16], U16, name="token_list")
        key_list = lists.tile([P, I // 16], U16, name="key_list")

        token_scales = keep.tile([P, PASSES, T], U8, name="token_scales")
        nc.vector.memset(token_scales[:].bitcast(I32), 0)

        rows_in = keep.tile([P, I], F32, name="rows_in")
        nc.gpsimd.memset(rows_in[:], 0.0)

        key_planes = {}
        for z, t0, count in ((0, 0, 2), (0, 2, 2), (1, 0, 2), (1, 2, 1), (1, 3, 1)):
            rows = ky[z * K_PASS : (z + 1) * K_PASS, :].rearrange("(p t) v -> p t v", t=PACK)
            planes = keep.tile([P, count, V], F32, name=f"key_planes_{z}_{t0}")
            nc.sync.dma_start(planes[:], rows[:, t0 : t0 + count, :])
            for t in range(count):
                key_planes[z, t0 + t] = planes[:, t, :]
            if (z, t0) == (0, 0):
                nc.sync.dma_start(key_list[:], offs2)
                nc.sync.dma_start(token_list[:], offs)
                nc.sync.dma_start(rows_in[0:1, :], bi)
                nc.sync.dma_start(rows_in[1:2, :], pr)
                nc.sync.dma_start(
                    token_scales[0:P:8, :, :].bitcast(I32),
                    xt_scales.rearrange("z q c -> q z c").bitcast(I32),
                )
        token_words = []
        for z in range(PASSES):
            words = keep.tile([P, T], I32, name=f"token_words_{z}")
            nc.sync.dma_start(words[:], xt_words[z].rearrange("p c r -> p (c r)").bitcast(I32))
            token_words.append(words)

        identity = keep.tile([P, P], F32, name="identity")
        make_identity(nc, identity[:])

        turned = psum.tile([P, 2, P], F32, name="turned")
        for h in range(2):
            nc.tensor.transpose(turned[:, h, :], rows_in[:, h * P : (h + 1) * P], identity[:])
        cols = keep.tile([P, 2, 2], F32, name="cols")
        nc.scalar.activation(cols[:], turned[:, :, 0:2], ACT.Copy)
        bias_rows = psum.tile([P, I], F32, name="bias_rows")
        prior = psum.tile([P, I], F32, name="prior")
        for which, spread in enumerate((bias_rows, prior)):
            for h in range(2):
                nc.tensor.transpose(
                    spread[:, h * P : (h + 1) * P],
                    cols[:, h, which : which + 1].to_broadcast([P, P]),
                    identity[:],
                )
        neg_bias = keep.tile([P, I], F32, name="neg_bias")
        nc.scalar.activation(neg_bias[:], bias_rows[:], ACT.Copy, scale=-GAIN)

        picked_scales = keep.tile([P, PASSES, J], U8, name="picked_scales")
        scale_planes = keep.tile([P, PASSES, J], U8, name="scale_planes", align_bytes=64)

        nc.gpsimd.memset(scale_planes[:].bitcast(I32), 0)
        for z in range(PASSES):
            nc.vector.tensor_copy(picked_scales[:, z, :], token_scales[:, z, :].indirect(token_list[:]))
        for q in range(0, P, 32):
            nc.vector.tensor_copy(
                scale_planes[q : q + 1, :, :].bitcast(I32), picked_scales[q : q + 1, :, :].bitcast(I32)
            )
        for r in range(1, 4):
            nc.scalar.dma_start(
                scale_planes[r:P:32, :, :].bitcast(I32), picked_scales[8 * r : P : 32, :, :].bitcast(I32)
            )

        key_codes, key_scales = [], []
        for z in range(PASSES):
            woven = keep.tile([P, I, PACK], BF16, name=f"woven_{z}", align_bytes=64)
            picked_keys = keep.tile([P, PACK, I], F32, name=f"picked_keys_{z}")
            codes = keep.tile([P, I], U32, name=f"key_codes_{z}", align_bytes=64)
            scales = keep.tile([P, I], U8, name=f"key_scales_{z}", align_bytes=64)
            last = z == PASSES - 1
            for t in range(PACK):
                window = key_planes[z, t]
                if last and t == PACK - 1:
                    nc.vector.tensor_copy(picked_keys[:, t, 0:P], window.indirect(key_list[:, 0:8]))
                    nc.scalar.activation(picked_keys[:, t, P:I], window.indirect(key_list[:, 8:16]), ACT.Copy)
                elif t % 2 == 0:
                    nc.scalar.activation(picked_keys[:, t, :], window.indirect(key_list[:]), ACT.Copy)
                else:
                    nc.vector.tensor_copy(picked_keys[:, t, :], window.indirect(key_list[:]))
            parts = [slice(0, P), slice(P, I)] if last else [slice(0, I)]
            for cols_i, weave in zip(parts, (nc.vector.tensor_copy, nc.scalar.copy)):
                weave(
                    woven[:, cols_i, :].rearrange("p (c i) t -> p c t i", i=4),
                    picked_keys[:, :, cols_i].rearrange("p t (c i) -> p c t i", i=4),
                )
            for cols_i in parts:
                nc.vector.quantize_mx(
                    out=codes[:, cols_i].bitcast(E4M3),
                    scales=scales[:, cols_i],
                    in_=woven[:, cols_i, :].rearrange("p i t -> p (i t)"),
                )
            key_codes.append(codes)
            key_scales.append(scales)

        scores = [psum.tile([P, I], F32, name=f"scores_{b}") for b in range(BLOCKS)]
        for z in range(PASSES):
            for b in range(BLOCKS):
                picked = keep.tile([P, P], U32, name=f"picked_words_{z}_{b}", align_bytes=64)
                nc.vector.tensor_copy(
                    picked[:], token_words[z][:].bitcast(U32).indirect(token_list[:, 8 * b : 8 * (b + 1)])
                )
                nc.tensor.matmul_mx(
                    out=scores[b][:],
                    lhsT=picked[:].bitcast(E5M2),
                    lhsT_scale=scale_planes[:, z, b * P : (b + 1) * P],
                    rhs=key_codes[z][:].bitcast(E4M3),
                    rhs_scale=key_scales[z][:],
                    start=(z == 0),
                    stop=(z == PASSES - 1),
                )

        def per_block(name, cols):
            return [keep.tile([P, cols], F32, name=f"{name}_{b}") for b in range(BLOCKS)]

        neg_logit, least, expo = per_block("neg_logit", I), per_block("least", 1), per_block("expo", I)
        terms, mean, inverse = per_block("terms", I), per_block("mean", 1), per_block("inverse", 1)
        centred, result = per_block("centred", I), per_block("result", I)
        for b in range(BLOCKS):
            nc.vector.scalar_tensor_tensor(
                neg_logit[b][:], scores[b][:], -GAIN, neg_bias[:], ALU.mult, ALU.add
            )
        for b in range(BLOCKS):
            nc.vector.tensor_reduce(least[b][:], neg_logit[b][:], mybir.AxisListType.X, ALU.min)
        for b in range(BLOCKS):
            nc.scalar.activation(expo[b][:], neg_logit[b][:], ACT.Exp, bias=least[b][:], scale=-1.0)
        for b in range(BLOCKS):
            nc.vector.scalar_tensor_tensor(
                terms[b][:], expo[b][:], 1.0 / SHARE, prior[:], ALU.mult, ALU.mult, accum_out=mean[b][:]
            )
        for b in range(BLOCKS):
            nc.vector.reciprocal(inverse[b][:], mean[b][:])
            nc.vector.scalar_tensor_tensor(
                centred[b][:], expo[b][:], mean[b][:], prior[:], ALU.subtract, ALU.mult
            )
        nc.scalar.activation(result[0][:], centred[0][:], ACT.Copy, scale=inverse[0][:])
        nc.vector.tensor_scalar(result[1][:], centred[1][:], inverse[1][:], None, ALU.mult)
        for b in range(BLOCKS):
            nc.sync.dma_start(out[b * P : (b + 1) * P, :], result[b][:])
